import numpy as np, ml_dtypes
CORES = [22,46,70,150,174,198,278,302,326,406,430,454]
N = 12
import mx_ref
NC, KT, G, ROOT = 128, 1, 2, 1
C = np.float32(0.041)
BF = ml_dtypes.bfloat16
def cut(t, i, w=512):
    return t[:, w * i:w * i + w]
def tile(rs):
    return np.stack(rs, axis=2).reshape(128, -1).astype(BF)
def layer(w, X):
    out = []
    for i in range(G):
        for t in range(len(X)):
            p = mx_ref.matmul(mx_ref.quantize(cut(w, len(X) * i + t)), X[t])
            z = p if t == 0 else z + p
        out.append(z)
    return out
def act(Z):
    return [np.maximum(s * z, 0) * C for z in Z for s in (1, -1)]
def setup_inputs(rng):
    def f(*shape):
        return mx_ref.flush((rng.standard_normal(shape, dtype=np.float32) * np.exp2(rng.integers(-2, 3, shape[:-1] + (1,)))).astype(BF))
    return {"x": f(N, 128, KT * 4 * NC), "w1": f(N, 128, G * KT * 512), "w2": f(N, 128, 512)}
def setup_inputs_blocks(rng):
    d = setup_inputs(rng)
    for k in ("x", "w1", "w2"): d[k] = mx_ref.spread(d[k], rng, 4)
    return d
def setup_inputs_wide(rng):
    d = setup_inputs(rng)
    for k in ("x", "w1", "w2"): d[k] = mx_ref.flush((d[k].astype(np.float32) * np.exp2(rng.integers(-8, 9, (N, 1, 1))).astype(np.float32)).astype(BF))
    return d
def setup_inputs_zeros(rng):
    d = setup_inputs(rng); v = d["x"].reshape(N, 128, -1, 4).copy()
    v[np.broadcast_to((rng.random((N, 1, v.shape[2], 1)) < 0.33), v.shape)] = 0
    d["x"] = v.reshape(d["x"].shape)
    return d
def reference(x, w1, w2):
    h = mx_ref.quantize(tile(act(layer(w1[ROOT], [mx_ref.quantize(cut(x[ROOT], t, 4 * NC)) for t in range(KT)]))))
    y = np.zeros((N, 128, NC), np.float32)
    for r in range(N):
        y[r] = mx_ref.matmul(mx_ref.quantize(w2[r]), h)
    return {"y": y}

@@ -1,0 +1,173 @@
+import numpy as np
+from concourse.bass import DstId, RemoteDMATransfer
+from concourse.mybir import dt, AluOpType, ActivationFunctionType
+
+COLS = 128
+GAIN = float(np.float32(0.041))
+
+SCRATCH = {
+    "xb": ("sbuf", [128, 4 * COLS], "bfloat16"),
+    "w1b": ("sbuf", [128, 1024], "bfloat16"),
+    "w2b": ("sbuf", [128, 512], "bfloat16"),
+    "hb": ("sbuf", [128, 4 * COLS], "bfloat16"),
+    "xq": ("sbuf", [128, COLS], "float8_e4m3fn_x4"),
+    "xs": ("sbuf", [128, COLS], "uint8"),
+    "w1q": ("sbuf", [128, 256], "float8_e4m3fn_x4"),
+    "w1s": ("sbuf", [128, 256], "uint8"),
+    "w2q": ("sbuf", [128, 128], "float8_e4m3fn_x4"),
+    "w2s": ("sbuf", [128, 128], "uint8"),
+    "hq": ("sbuf", [128, COLS], "float8_e4m3fn_x4"),
+    "hs": ("sbuf", [128, COLS], "uint8"),
+    "yb": ("sbuf", [128, COLS], "float32"),
+    "ps": ("psum", [128, 3 * 512], "float32"),
+}
+SEMAPHORES = ["ld_x", "ld_w1", "ld_w2", "q_in", "q_w2", "mm0", "mm1", "act", "q_h",
+              "arr_p", "arr_c", "sent", "mm_y", "cp_y", "st_y"]
+
+
+def _bits(mask):
+    return [b for b in range(mask.bit_length()) if (mask >> b) & 1]
+
+
+def _plan(T, topo):
+    ranks = list(T.cores)
+    root = ranks[T.root]
+
+    def rack(c):
+        return topo.rack(topo.host(c))
+
+    def engines(src, dsts):
+        m = topo.mask(src, dsts[0])
+        for d in dsts[1:]:
+            m &= topo.mask(src, d)
+        return _bits(m)
+
+    others = [c for c in ranks if c != root]
+    far = [c for c in others if not topo.may_write(root, c)]
+    near = [c for c in others if topo.may_write(root, c)]
+    in_rack = [c for c in near if rack(c) == rack(far[0]) and topo.chip(c) == topo.chip(root)][0]
+    cabled = [c for c in near if topo.same_plane(root, c)][0]
+    straight = [c for c in far if topo.chip(c) == topo.chip(cabled)][0]
+    bent = [c for c in far if c != straight]
+    rest = [c for c in near if c not in (in_rack, cabled)]
+    own = [c for c in rest if topo.host(c) == topo.host(root)]
+    side = [c for c in rest if topo.host(c) != topo.host(root) and rack(c) == rack(root)]
+    over = [c for c in rest if rack(c) != rack(root)]
+    leaves = own + side[:1]
+    e1, e2, e3 = side[1], over[1], over[0]
+    span = topo.CORES_PER_CHIP
+    able = [c for c in range(max(root - span, 0), root + span)
+            if c != root and T.rank_of(c) is None and topo.host(c) == topo.host(root) and topo.chip(c) == topo.chip(root)
+            and all(topo.may_write(c, d) for d in (e1, e2, e3))]
+    h_same = [c for c in able if topo.die(c) == topo.die(root)][0]
+    h_other = [c for c in able if topo.die(c) != topo.die(root)][0]
+
+    out = engines(root, [in_rack, cabled] + leaves)
+    inner = [b for b in engines(root, [h_same, h_other]) if b not in out]
+
+    def pair(a, b, da, dab, db):
+        return {a: [("P", [(engines(a, [da]), [da])]), ("C", [(engines(a, [da, dab]), [da, dab])])],
+                b: [("P", [(engines(b, [db, dab]), [db, dab])]), ("C", [(engines(b, [db]), [db])])]}
+
+    plan = {root: [("P", [(out, [in_rack, cabled])]),
+                   ("P", [(inner, [h_same, h_other])]),
+                   ("C", [(out, [in_rack, cabled])]),
+                   ("C", [(inner, [h_same, h_other])]),
+                   ("P", [(out, leaves)]),
+                   ("C", [(out, leaves)])]}
+    plan.update(pair(in_rack, cabled, bent[0], bent[1], straight))
+    plan.update(pair(h_same, h_other, e1, e2, e3))
+    return root, plan
+
+
+def _lands(plan, core):
+    n = {"P": 0, "C": 0}
+    for calls in plan.values():
+        for piece, groups in calls:
+            for eng, dsts in groups:
+                n[piece] += len(eng) * dsts.count(core)
+    return n
+
+
+def _send_all(g, core, T, topo, calls, lands):
+    s = T.sem
+    have = set()
+    left = 0
+    for piece, groups in calls:
+        if lands[piece] and piece not in have:
+            g.wait_ge(s.arr_p if piece == "P" else s.arr_c, lands[piece])
+            have.add(piece)
+        trs = []
+        for eng, dsts in groups:
+            ids = []
+            for d in dsts:
+                rid, pid = topo.addr(d, core)
+                ids.append(DstId(rid=rid, pnc=pid))
+            if piece == "P":
+                src, dst, sem = T.hs[:], [T.hs[:] for _ in dsts], s.arr_p
+            else:
+                src, dst, sem = T.hq[:].bitcast(dt.uint8), [T.hq[:].bitcast(dt.uint8) for _ in dsts], s.arr_c
+            trs.append(RemoteDMATransfer(dst_ids=ids, dma_engine_mask=sum(1 << b for b in eng), remote_sem=sem,
+                                         srcs=[src], dsts=dst))
+            left += len(eng)
+        g.remote_dma_fused(trs, local_sem=s.sent)
+    g.wait_ge(s.sent, left)
+
+
+def _make_h(g, T):
+    s = T.sem
+    z0, z1 = T.ps[:, 0:COLS], T.ps[:, 512:512 + COLS]
+    g.sync.dma_start(T.xb[:], T.x[:]).then_inc(s.ld_x, 16)
+    g.scalar.dma_start(T.w1b[:], T.w1[:]).then_inc(s.ld_w1, 16)
+    g.vector.wait_ge(s.ld_x, 16)
+    g.vector.quantize_mx(T.xq[:], T.xs[:], T.xb[:]).then_inc(s.q_in, 1)
+    g.vector.wait_ge(s.ld_w1, 16)
+    g.vector.quantize_mx(T.w1q[:], T.w1s[:], T.w1b[:]).then_inc(s.q_in, 1)
+    g.tensor.wait_ge(s.q_in, 2)
+    g.tensor.matmul_mx(z0, T.w1q[:, 0:128], T.w1s[:, 0:128], T.xq[:], T.xs[:], True, True).then_inc(s.mm0, 1)
+    g.tensor.matmul_mx(z1, T.w1q[:, 128:256], T.w1s[:, 128:256], T.xq[:], T.xs[:], True, True).then_inc(s.mm1, 1)
+    n = 4 * COLS
+    g.vector.wait_ge(s.mm0, 1)
+    g.vector.tensor_scalar(T.hb[:, 0:n:4], z0, GAIN, 0.0, AluOpType.mult, AluOpType.max).then_inc(s.act, 1)
+    g.vector.tensor_scalar(T.hb[:, 1:n:4], z0, -GAIN, 0.0, AluOpType.mult, AluOpType.max).then_inc(s.act, 1)
+    g.scalar.wait_ge(s.mm1, 1)
+    g.scalar.activation(T.hb[:, 2:n:4], z1, ActivationFunctionType.Relu, scale=GAIN).then_inc(s.act, 1)
+    g.scalar.activation(T.hb[:, 3:n:4], z1, ActivationFunctionType.Relu, scale=-GAIN).then_inc(s.act, 1)
+    g.vector.wait_ge(s.act, 4)
+    g.vector.quantize_mx(T.hq[:], T.hs[:], T.hb[:]).then_inc(s.q_h, 1)
+
+
+def rank_program(g, core, T, topo):
+    root, plan = _plan(T, topo)
+    rank = T.rank_of(core)
+    calls = plan.get(core, [])
+    if rank is None and not calls:
+        return
+    s = T.sem
+    lands = _lands(plan, core)
+
+    if core == root:
+        _make_h(g, T)
+        g.sync.wait_ge(s.ld_w1, 16)
+    if rank is not None:
+        g.sync.dma_start(T.w2b[:], T.w2[:]).then_inc(s.ld_w2, 16)
+        g.vector.wait_ge(s.ld_w2, 16)
+        g.vector.quantize_mx(T.w2q[:], T.w2s[:], T.w2b[:]).then_inc(s.q_w2, 1)
+        py = T.ps[:, 1024:1024 + COLS]
+        g.tensor.wait_ge(s.q_w2, 1)
+        if core == root:
+            g.tensor.wait_ge(s.q_h, 1)
+        else:
+            g.tensor.wait_ge(s.arr_p, lands["P"])
+            g.tensor.wait_ge(s.arr_c, lands["C"])
+        g.tensor.matmul_mx(py, T.w2q[:], T.w2s[:], T.hq[:], T.hs[:], True, True).then_inc(s.mm_y, 1)
+        g.vector.wait_ge(s.mm_y, 1)
+        g.vector.tensor_copy(T.yb[:], py).then_inc(s.cp_y, 1)
+        g.sync.wait_ge(s.cp_y, 1)
+        g.sync.dma_start(T.y[:], T.yb[:]).then_inc(s.st_y, 16)
+        g.sync.wait_ge(s.st_y, 16)
+
+    if calls:
+        if core == root:
+            g.wait_ge(s.q_h, 1)
+        _send_all(g, core, T, topo, calls, lands)

@@ -11,9 +11,8 @@ SCRATCH = {
     "w2b": ("sbuf", [128, 512], "bfloat16"),
     "hb": ("sbuf", [128, 4 * COLS], "bfloat16"),
     "xq": ("sbuf", [128, COLS], "float8_e4m3fn_x4"),
-    "xs": ("sbuf", [128, COLS], "uint8"),
     "w1q": ("sbuf", [128, 256], "float8_e4m3fn_x4"),
-    "w1s": ("sbuf", [128, 256], "uint8"),
+    "s1": ("sbuf", [128, COLS + 256], "uint8"),
     "w2q": ("sbuf", [128, 128], "float8_e4m3fn_x4"),
     "w2s": ("sbuf", [128, 128], "uint8"),
     "hq": ("sbuf", [128, COLS], "float8_e4m3fn_x4"),
@@ -21,8 +20,8 @@ SCRATCH = {
     "yb": ("sbuf", [128, COLS], "float32"),
     "ps": ("psum", [128, 3 * 512], "float32"),
 }
-SEMAPHORES = ["ld_x", "ld_w1", "ld_w2", "q_in", "q_w2", "mm0", "mm1", "act", "q_h",
-              "arr_p", "arr_c", "sent", "mm_y", "cp_y", "st_y"]
+SEMAPHORES = ["ld_x", "ld_w1", "ld_w2", "q_x", "q_wa", "q_wb", "q_w2", "mm0", "mm1", "act", "q_h",
+              "arr_x", "arr_w", "arr_p", "arr_c", "sent", "mm_y", "cp_y", "st_y"]
 
 
 def _bits(mask):
@@ -53,31 +52,31 @@ def _plan(T, topo):
     own = [c for c in rest if topo.host(c) == topo.host(root)]
     side = [c for c in rest if topo.host(c) != topo.host(root) and rack(c) == rack(root)]
     over = [c for c in rest if rack(c) != rack(root)]
-    leaves = own + side[:1]
-    e1, e2, e3 = side[1], over[1], over[0]
     span = topo.CORES_PER_CHIP
     able = [c for c in range(max(root - span, 0), root + span)
             if c != root and T.rank_of(c) is None and topo.host(c) == topo.host(root) and topo.chip(c) == topo.chip(root)
-            and all(topo.may_write(c, d) for d in (e1, e2, e3))]
-    h_same = [c for c in able if topo.die(c) == topo.die(root)][0]
-    h_other = [c for c in able if topo.die(c) != topo.die(root)][0]
+            and all(topo.may_write(c, d) for d in rest)]
+    twin = [c for c in able if topo.die(c) == topo.die(root)][0]
+    h_a, h_b = [c for c in able if topo.die(c) != topo.die(root)][:2]
 
-    out = engines(root, [in_rack, cabled] + leaves)
-    inner = [b for b in engines(root, [h_same, h_other]) if b not in out]
+    out = engines(root, [in_rack, cabled] + own)
+    inner = [b for b in engines(root, [h_a, h_b]) if b not in out]
 
     def pair(a, b, da, dab, db):
         return {a: [("P", [(engines(a, [da]), [da])]), ("C", [(engines(a, [da, dab]), [da, dab])])],
                 b: [("P", [(engines(b, [db, dab]), [db, dab])]), ("C", [(engines(b, [db]), [db])])]}
 
     plan = {root: [("P", [(out, [in_rack, cabled])]),
-                   ("P", [(inner, [h_same, h_other])]),
+                   ("P", [(inner, [h_a, h_b])]),
                    ("C", [(out, [in_rack, cabled])]),
-                   ("C", [(inner, [h_same, h_other])]),
-                   ("P", [(out, leaves)]),
-                   ("C", [(out, leaves)])]}
+                   ("C", [(inner, [h_a, h_b])]),
+                   ("P", [(out, own)]),
+                   ("C", [(out, own)])],
+            twin: [("P", [(engines(twin, over[:1]), over[:1])]),
+                   ("C", [(engines(twin, over[:1]), over[:1])])]}
     plan.update(pair(in_rack, cabled, bent[0], bent[1], straight))
-    plan.update(pair(h_same, h_other, e1, e2, e3))
-    return root, plan
+    plan.update(pair(h_a, h_b, side[0], side[1], over[1]))
+    return root, twin, plan
 
 
 def _lands(plan, core):
@@ -89,43 +88,42 @@ def _lands(plan, core):
     return n
 
 
-def _send_all(g, core, T, topo, calls, lands):
+def _call(g, core, T, topo, view, sem, groups):
+    trs, left = [], 0
+    for eng, dsts in groups:
+        ids = []
+        for d in dsts:
+            rid, pid = topo.addr(d, core)
+            ids.append(DstId(rid=rid, pnc=pid))
+        trs.append(RemoteDMATransfer(dst_ids=ids, dma_engine_mask=sum(1 << b for b in eng), remote_sem=sem,
+                                     srcs=[view()], dsts=[view() for _ in dsts]))
+        left += len(eng)
+    g.remote_dma_fused(trs, local_sem=T.sem.sent)
+    return left
+
+
+def _send_h(g, core, T, topo, calls, lands, left):
     s = T.sem
     have = set()
-    left = 0
     for piece, groups in calls:
         if lands[piece] and piece not in have:
             g.wait_ge(s.arr_p if piece == "P" else s.arr_c, lands[piece])
             have.add(piece)
-        trs = []
-        for eng, dsts in groups:
-            ids = []
-            for d in dsts:
-                rid, pid = topo.addr(d, core)
-                ids.append(DstId(rid=rid, pnc=pid))
-            if piece == "P":
-                src, dst, sem = T.hs[:], [T.hs[:] for _ in dsts], s.arr_p
-            else:
-                src, dst, sem = T.hq[:].bitcast(dt.uint8), [T.hq[:].bitcast(dt.uint8) for _ in dsts], s.arr_c
-            trs.append(RemoteDMATransfer(dst_ids=ids, dma_engine_mask=sum(1 << b for b in eng), remote_sem=sem,
-                                         srcs=[src], dsts=dst))
-            left += len(eng)
-        g.remote_dma_fused(trs, local_sem=s.sent)
+        if piece == "P":
+            left += _call(g, core, T, topo, lambda: T.hs[:], s.arr_p, groups)
+        else:
+            left += _call(g, core, T, topo, lambda: T.hq[:].bitcast(dt.uint8), s.arr_c, groups)
     g.wait_ge(s.sent, left)
 
 
-def _make_h(g, T):
+def _layer1(g, T, gate=None):
     s = T.sem
     z0, z1 = T.ps[:, 0:COLS], T.ps[:, 512:512 + COLS]
-    g.sync.dma_start(T.xb[:], T.x[:]).then_inc(s.ld_x, 16)
-    g.scalar.dma_start(T.w1b[:], T.w1[:]).then_inc(s.ld_w1, 16)
-    g.vector.wait_ge(s.ld_x, 16)
-    g.vector.quantize_mx(T.xq[:], T.xs[:], T.xb[:]).then_inc(s.q_in, 1)
-    g.vector.wait_ge(s.ld_w1, 16)
-    g.vector.quantize_mx(T.w1q[:], T.w1s[:], T.w1b[:]).then_inc(s.q_in, 1)
-    g.tensor.wait_ge(s.q_in, 2)
-    g.tensor.matmul_mx(z0, T.w1q[:, 0:128], T.w1s[:, 0:128], T.xq[:], T.xs[:], True, True).then_inc(s.mm0, 1)
-    g.tensor.matmul_mx(z1, T.w1q[:, 128:256], T.w1s[:, 128:256], T.xq[:], T.xs[:], True, True).then_inc(s.mm1, 1)
+    xs, wa, wb = T.s1[:, 0:COLS], T.s1[:, COLS:COLS + 128], T.s1[:, COLS + 128:COLS + 256]
+    g.tensor.matmul_mx(z0, T.w1q[:, 0:128], wa, T.xq[:], xs, True, True).then_inc(s.mm0, 1)
+    if gate is not None:
+        g.tensor.wait_ge(gate, 1)
+    g.tensor.matmul_mx(z1, T.w1q[:, 128:256], wb, T.xq[:], xs, True, True).then_inc(s.mm1, 1)
     n = 4 * COLS
     g.vector.wait_ge(s.mm0, 1)
     g.vector.tensor_scalar(T.hb[:, 0:n:4], z0, GAIN, 0.0, AluOpType.mult, AluOpType.max).then_inc(s.act, 1)
@@ -138,17 +136,40 @@ def _make_h(g, T):
 
 
 def rank_program(g, core, T, topo):
-    root, plan = _plan(T, topo)
+    root, twin, plan = _plan(T, topo)
     rank = T.rank_of(core)
     calls = plan.get(core, [])
     if rank is None and not calls:
         return
     s = T.sem
     lands = _lands(plan, core)
+    left = 0
+    whole = _bits(topo.mask(root, twin))
 
     if core == root:
-        _make_h(g, T)
+        g.sync.dma_start(T.xb[:], T.x[:]).then_inc(s.ld_x, 16)
+        g.scalar.dma_start(T.w1b[:], T.w1[:]).then_inc(s.ld_w1, 16)
+        g.vector.wait_ge(s.ld_x, 16)
+        g.vector.quantize_mx(T.xq[:], T.s1[:, 0:COLS], T.xb[:]).then_inc(s.q_x, 1)
+        g.vector.wait_ge(s.ld_w1, 16)
+        g.vector.quantize_mx(T.w1q[:, 0:128], T.s1[:, COLS:COLS + 128], T.w1b[:, 0:512]).then_inc(s.q_wa, 1)
+        g.vector.quantize_mx(T.w1q[:, 128:256], T.s1[:, COLS + 128:COLS + 256], T.w1b[:, 512:1024]).then_inc(s.q_wb, 1)
+        g.tensor.wait_ge(s.q_x, 1)
+        g.tensor.wait_ge(s.q_wa, 1)
+        _layer1(g, T, s.q_wb)
+        to_twin = [(whole, [twin])]
+        g.wait_ge(s.q_x, 1)
+        left += _call(g, core, T, topo, lambda: T.xq[:].bitcast(dt.uint8), s.arr_x, to_twin)
+        g.wait_ge(s.q_wa, 1)
+        g.wait_ge(s.q_wb, 1)
+        left += _call(g, core, T, topo, lambda: T.s1[:], s.arr_w, to_twin)
+        left += _call(g, core, T, topo, lambda: T.w1q[:].bitcast(dt.uint8), s.arr_w, to_twin)
         g.sync.wait_ge(s.ld_w1, 16)
+    if core == twin:
+        g.tensor.wait_ge(s.arr_x, len(whole))
+        g.tensor.wait_ge(s.arr_w, 2 * len(whole))
+        _layer1(g, T)
+
     if rank is not None:
         g.sync.dma_start(T.w2b[:], T.w2[:]).then_inc(s.ld_w2, 16)
         g.vector.wait_ge(s.ld_w2, 16)
@@ -168,6 +189,6 @@ def rank_program(g, core, T, topo):
         g.sync.wait_ge(s.st_y, 16)
 
     if calls:
-        if core == root:
+        if core in (root, twin):
             g.wait_ge(s.q_h, 1)
-        _send_all(g, core, T, topo, calls, lands)
+        _send_h(g, core, T, topo, calls, lands, left)

import numpy as np
from concourse.bass import DstId, RemoteDMATransfer
from concourse.mybir import dt, AluOpType, ActivationFunctionType

COLS = 128
GAIN = float(np.float32(0.041))

SCRATCH = {
    "xb": ("sbuf", [128, 4 * COLS], "bfloat16"),
    "w1b": ("sbuf", [128, 1024], "bfloat16"),
    "w2b": ("sbuf", [128, 512], "bfloat16"),
    "hb": ("sbuf", [128, 4 * COLS], "bfloat16"),
    "xq": ("sbuf", [128, COLS], "float8_e4m3fn_x4"),
    "w1q": ("sbuf", [128, 256], "float8_e4m3fn_x4"),
    "s1": ("sbuf", [128, COLS + 256], "uint8"),
    "w2q": ("sbuf", [128, 128], "float8_e4m3fn_x4"),
    "w2s": ("sbuf", [128, 128], "uint8"),
    "hq": ("sbuf", [128, COLS], "float8_e4m3fn_x4"),
    "hs": ("sbuf", [128, COLS], "uint8"),
    "yb": ("sbuf", [128, COLS], "float32"),
    "ps": ("psum", [128, 3 * 512], "float32"),
}
SEMAPHORES = ["ld_x", "ld_w1", "ld_w2", "q_x", "q_wa", "q_wb", "q_w2", "mm0", "mm1", "act", "q_h",
              "arr_x", "arr_w", "arr_p", "arr_c", "sent", "mm_y", "cp_y", "st_y"]


def _bits(mask):
    return [b for b in range(mask.bit_length()) if (mask >> b) & 1]


def _plan(T, topo):
    ranks = list(T.cores)
    root = ranks[T.root]

    def rack(c):
        return topo.rack(topo.host(c))

    def engines(src, dsts):
        m = topo.mask(src, dsts[0])
        for d in dsts[1:]:
            m &= topo.mask(src, d)
        return _bits(m)

    others = [c for c in ranks if c != root]
    far = [c for c in others if not topo.may_write(root, c)]
    near = [c for c in others if topo.may_write(root, c)]
    in_rack = [c for c in near if rack(c) == rack(far[0]) and topo.chip(c) == topo.chip(root)][0]
    cabled = [c for c in near if topo.same_plane(root, c)][0]
    straight = [c for c in far if topo.chip(c) == topo.chip(cabled)][0]
    bent = [c for c in far if c != straight]
    rest = [c for c in near if c not in (in_rack, cabled)]
    own = [c for c in rest if topo.host(c) == topo.host(root)]
    side = [c for c in rest if topo.host(c) != topo.host(root) and rack(c) == rack(root)]
    over = [c for c in rest if rack(c) != rack(root)]
    span = topo.CORES_PER_CHIP
    able = [c for c in range(max(root - span, 0), root + span)
            if c != root and T.rank_of(c) is None and topo.host(c) == topo.host(root) and topo.chip(c) == topo.chip(root)
            and all(topo.may_write(c, d) for d in rest)]
    twin = [c for c in able if topo.die(c) == topo.die(root)][0]
    h_a, h_b = [c for c in able if topo.die(c) != topo.die(root)][:2]

    out = engines(root, [in_rack, cabled] + own)
    inner = [b for b in engines(root, [h_a, h_b]) if b not in out]

    def pair(a, b, da, dab, db):
        return {a: [("P", [(engines(a, [da]), [da])]), ("C", [(engines(a, [da, dab]), [da, dab])])],
                b: [("P", [(engines(b, [db, dab]), [db, dab])]), ("C", [(engines(b, [db]), [db])])]}

    plan = {root: [("P", [(out, [in_rack, cabled])]),
                   ("P", [(inner, [h_a, h_b])]),
                   ("C", [(out, [in_rack, cabled])]),
                   ("C", [(inner, [h_a, h_b])]),
                   ("P", [(out, own)]),
                   ("C", [(out, own)])],
            twin: [("P", [(engines(twin, over[:1]), over[:1])]),
                   ("C", [(engines(twin, over[:1]), over[:1])])]}
    plan.update(pair(in_rack, cabled, bent[0], bent[1], straight))
    plan.update(pair(h_a, h_b, side[0], side[1], over[1]))
    return root, twin, plan


def _lands(plan, core):
    n = {"P": 0, "C": 0}
    for calls in plan.values():
        for piece, groups in calls:
            for eng, dsts in groups:
                n[piece] += len(eng) * dsts.count(core)
    return n


def _call(g, core, T, topo, view, sem, groups):
    trs, left = [], 0
    for eng, dsts in groups:
        ids = []
        for d in dsts:
            rid, pid = topo.addr(d, core)
            ids.append(DstId(rid=rid, pnc=pid))
        trs.append(RemoteDMATransfer(dst_ids=ids, dma_engine_mask=sum(1 << b for b in eng), remote_sem=sem,
                                     srcs=[view()], dsts=[view() for _ in dsts]))
        left += len(eng)
    g.remote_dma_fused(trs, local_sem=T.sem.sent)
    return left


def _send_h(g, core, T, topo, calls, lands, left):
    s = T.sem
    have = set()
    for piece, groups in calls:
        if lands[piece] and piece not in have:
            g.wait_ge(s.arr_p if piece == "P" else s.arr_c, lands[piece])
            have.add(piece)
        if piece == "P":
            left += _call(g, core, T, topo, lambda: T.hs[:], s.arr_p, groups)
        else:
            left += _call(g, core, T, topo, lambda: T.hq[:].bitcast(dt.uint8), s.arr_c, groups)
    g.wait_ge(s.sent, left)


def _layer1(g, T, gate=None):
    s = T.sem
    z0, z1 = T.ps[:, 0:COLS], T.ps[:, 512:512 + COLS]
    xs, wa, wb = T.s1[:, 0:COLS], T.s1[:, COLS:COLS + 128], T.s1[:, COLS + 128:COLS + 256]
    g.tensor.matmul_mx(z0, T.w1q[:, 0:128], wa, T.xq[:], xs, True, True).then_inc(s.mm0, 1)
    if gate is not None:
        g.tensor.wait_ge(gate, 1)
    g.tensor.matmul_mx(z1, T.w1q[:, 128:256], wb, T.xq[:], xs, True, True).then_inc(s.mm1, 1)
    n = 4 * COLS
    g.vector.wait_ge(s.mm0, 1)
    g.vector.tensor_scalar(T.hb[:, 0:n:4], z0, GAIN, 0.0, AluOpType.mult, AluOpType.max).then_inc(s.act, 1)
    g.vector.tensor_scalar(T.hb[:, 1:n:4], z0, -GAIN, 0.0, AluOpType.mult, AluOpType.max).then_inc(s.act, 1)
    g.scalar.wait_ge(s.mm1, 1)
    g.scalar.activation(T.hb[:, 2:n:4], z1, ActivationFunctionType.Relu, scale=GAIN).then_inc(s.act, 1)
    g.scalar.activation(T.hb[:, 3:n:4], z1, ActivationFunctionType.Relu, scale=-GAIN).then_inc(s.act, 1)
    g.vector.wait_ge(s.act, 4)
    g.vector.quantize_mx(T.hq[:], T.hs[:], T.hb[:]).then_inc(s.q_h, 1)


def rank_program(g, core, T, topo):
    root, twin, plan = _plan(T, topo)
    rank = T.rank_of(core)
    calls = plan.get(core, [])
    if rank is None and not calls:
        return
    s = T.sem
    lands = _lands(plan, core)
    left = 0
    whole = _bits(topo.mask(root, twin))

    if core == root:
        g.sync.dma_start(T.xb[:], T.x[:]).then_inc(s.ld_x, 16)
        g.scalar.dma_start(T.w1b[:], T.w1[:]).then_inc(s.ld_w1, 16)
        g.vector.wait_ge(s.ld_x, 16)
        g.vector.quantize_mx(T.xq[:], T.s1[:, 0:COLS], T.xb[:]).then_inc(s.q_x, 1)
        g.vector.wait_ge(s.ld_w1, 16)
        g.vector.quantize_mx(T.w1q[:, 0:128], T.s1[:, COLS:COLS + 128], T.w1b[:, 0:512]).then_inc(s.q_wa, 1)
        g.vector.quantize_mx(T.w1q[:, 128:256], T.s1[:, COLS + 128:COLS + 256], T.w1b[:, 512:1024]).then_inc(s.q_wb, 1)
        g.tensor.wait_ge(s.q_x, 1)
        g.tensor.wait_ge(s.q_wa, 1)
        _layer1(g, T, s.q_wb)
        to_twin = [(whole, [twin])]
        g.wait_ge(s.q_x, 1)
        left += _call(g, core, T, topo, lambda: T.xq[:].bitcast(dt.uint8), s.arr_x, to_twin)
        g.wait_ge(s.q_wa, 1)
        g.wait_ge(s.q_wb, 1)
        left += _call(g, core, T, topo, lambda: T.s1[:], s.arr_w, to_twin)
        left += _call(g, core, T, topo, lambda: T.w1q[:].bitcast(dt.uint8), s.arr_w, to_twin)
        g.sync.wait_ge(s.ld_w1, 16)
    if core == twin:
        g.tensor.wait_ge(s.arr_x, len(whole))
        g.tensor.wait_ge(s.arr_w, 2 * len(whole))
        _layer1(g, T)

    if rank is not None:
        g.sync.dma_start(T.w2b[:], T.w2[:]).then_inc(s.ld_w2, 16)
        g.vector.wait_ge(s.ld_w2, 16)
        g.vector.quantize_mx(T.w2q[:], T.w2s[:], T.w2b[:]).then_inc(s.q_w2, 1)
        py = T.ps[:, 1024:1024 + COLS]
        g.tensor.wait_ge(s.q_w2, 1)
        if core == root:
            g.tensor.wait_ge(s.q_h, 1)
        else:
            g.tensor.wait_ge(s.arr_p, lands["P"])
            g.tensor.wait_ge(s.arr_c, lands["C"])
        g.tensor.matmul_mx(py, T.w2q[:], T.w2s[:], T.hq[:], T.hs[:], True, True).then_inc(s.mm_y, 1)
        g.vector.wait_ge(s.mm_y, 1)
        g.vector.tensor_copy(T.yb[:], py).then_inc(s.cp_y, 1)
        g.sync.wait_ge(s.cp_y, 1)
        g.sync.dma_start(T.y[:], T.yb[:]).then_inc(s.st_y, 16)
        g.sync.wait_ge(s.st_y, 16)

    if calls:
        if core in (root, twin):
            g.wait_ge(s.q_h, 1)
        _send_h(g, core, T, topo, calls, lands, left)
